import numpy as np
import ml_dtypes


def mxq(x, axis, fmt="e4m3"):
    dtype, down = {"e4m3": (ml_dtypes.float8_e4m3fn, 7), "e5m2": (ml_dtypes.float8_e5m2, 14)}[fmt]
    v = np.moveaxis(np.asarray(x, np.float32).astype(ml_dtypes.bfloat16).astype(np.float64), axis, -1)
    blocks = v.reshape(v.shape[:-1] + (-1, 32))
    amax = np.abs(blocks).max(-1, keepdims=True)
    byte = np.maximum(np.where(amax > 0, np.frexp(amax)[1] - 1 + 127, 0) - down, 1)
    scale = np.exp2(byte - 127.0)
    codes = (blocks / scale).astype(np.float32).astype(dtype).astype(np.float64)
    return np.moveaxis((codes * scale).reshape(v.shape), -1, axis)


WIDE = False


def mx_kscale(k):
    if not WIDE:
        return np.ones(k)
    levels = np.array([10, -10, 5, -5, 0])
    if k % 512:
        return np.exp2(np.random.permutation(np.resize(levels, k // 32))).repeat(32)
    a = np.empty((k // 512, 16))
    for p in range(k // 512):
        a[p, :8] = np.random.permutation(np.resize(levels, 8))
        for g in range(8):
            far = levels[np.abs(levels - a[p, g]) >= 10]
            a[p, g + 8] = far[np.random.randint(len(far))]
    return np.exp2(a.ravel()).repeat(32)


def f64(x):
    return np.asarray(x).astype(np.float64)


def striped(idx):
    return np.tile(idx.reshape(-1, 16).T, (8, 1)).astype(np.uint16)


def unstriped(offs):
    return offs[:16].T.reshape(-1).astype(np.int64)


E2M1 = np.array([0.0, 0.5, 1.0, 1.5, 2.0, 3.0, 4.0, 6.0, -0.0, -0.5, -1.0, -1.5, -2.0, -3.0, -4.0, -6.0])


def pack_weight(w, fmt):
    k, n = w.shape
    w = f64(np.asarray(w, np.float32).astype(ml_dtypes.bfloat16)).reshape(k // 32, 32, n)
    amax = np.abs(w).max(1)
    if fmt == "e4m3":
        byte = np.frexp(amax)[1] - 1 + 127 - 7
    else:
        mant, ex = np.frexp(amax / 6.0)
        byte = np.where(mant > 0.5, ex, ex - 1) + 127
    byte = np.clip(np.where(amax > 0, byte, 1), 1, 254)
    scaled = (w * np.exp2(127.0 - byte)[:, None, :]).reshape(k, n).astype(np.float32)
    by_word = np.ascontiguousarray(scaled.reshape(k // 512, 128, 4, n).transpose(0, 1, 3, 2))
    if fmt == "e4m3":
        words = by_word.astype(ml_dtypes.float8_e4m3fn).view(np.uint8)
    else:
        c = by_word.astype(ml_dtypes.float4_e2m1fn).view(np.uint8) & 0xF
        words = (c[..., 0::2] | (c[..., 1::2] << 4)).reshape(k // 512, 128, 2 * n)
    return np.ascontiguousarray(words), np.ascontiguousarray(byte.astype(np.uint8).reshape(k // 512, 16, n))


def unpack_weight(words, scales, fmt):
    g, _, n = scales.shape
    words = np.ascontiguousarray(words).reshape(g, 128, n, -1)
    if fmt == "e4m3":
        vals = words.view(ml_dtypes.float8_e4m3fn).astype(np.float64)
    else:
        nib = np.empty((g, 128, n, 4), np.uint8)
        nib[..., 0::2] = words & 0xF
        nib[..., 1::2] = words >> 4
        vals = E2M1[nib]
    vals = vals * np.repeat(np.exp2(scales.astype(np.float64) - 127.0), 8, axis=1)[..., None]
    return vals.transpose(0, 1, 3, 2).reshape(g * 512, n)


def gelu(v):
    return 0.5 * v * (1.0 + np.tanh(np.sqrt(2.0 / np.pi) * (v + 0.044715 * v**3)))


K, M, H, N, T, S, T2, P = 1024, 512, 1024, 512, 2048, 512, 2048, 1024

def setup_inputs():
    n = np.random.standard_normal
    s, s2, u = mx_kscale(K)[:, None], mx_kscale(M)[:, None], mx_kscale(H)[:, None]
    d = {}
    d["tab_words"], d["tab_scales"] = pack_weight(np.random.uniform(-1.7, 1.7, (K, T)) * s, "e4m3")
    d["offs"] = striped(np.random.permutation(T)[:S])
    d["tab2_words"], d["tab2_scales"] = pack_weight(n((M, T)) * s2, "e4m3")
    d["offs2"] = striped(np.random.permutation(T)[:S])
    skip = np.eye(K, H) * np.random.uniform(0.7, 0.9, (1, H))
    d["w1"] = ((0.24 * n((K, H)) / K**0.5 + skip) / s).astype(np.float32)
    d["gain"] = (np.random.uniform(1.5, 3.0, H) * u[:, 0]).astype(np.float32)
    d["w2_words"], d["w2_scales"] = pack_weight(4.0 * n((M, H)) / M**0.5 / s2 * u.T**2, "e2m1")
    d["page0"] = (0.7 * n((H, T2)) * u).astype(np.float32)
    d["wg1"] = np.exp(0.3 * n((128, S))).astype(np.float32)
    d["wg2"] = np.exp(0.3 * n((128, S))).astype(np.float32)
    perm = np.random.permutation(T2)
    d["offs3"] = striped(perm[:S])
    d["offs4"] = striped(perm[S:2 * S])
    d["offs5"] = striped(np.random.permutation(T2)[:P])
    d["base"] = (0.6 * n(H) * u[:, 0]).astype(np.float32)
    d["w3"] = (0.6 * n((H, N)) / H**0.5 / u).astype(np.float32)
    d["plan"] = (n((M, P)) * s2).astype(np.float32)
    d["w4_words"], d["w4_scales"] = pack_weight(2.0 * n((M, N)) / M**0.5 / s2, "e4m3")
    return d

def reference(tab_words, tab_scales, offs, tab2_words, tab2_scales, offs2, w1, gain, w2_words, w2_scales, page0, wg1, wg2, offs3, offs4, offs5, base, w3, plan, w4_words, w4_scales):
    v = unpack_weight(tab_words, tab_scales, "e4m3")[:, unstriped(offs)]
    v2 = unpack_weight(tab2_words, tab2_scales, "e4m3")[:, unstriped(offs2)]
    h1 = f64(gain)[:, None] * np.sin(mxq(f64(w1), 0, "e4m3").T @ v)
    h2 = np.sqrt(np.abs(unpack_weight(w2_words, w2_scales, "e2m1").T @ v2))
    page = f64(page0).copy()
    page[:, unstriped(offs3)] = np.tile(f64(wg1), (H // 128, 1)) * h1
    page[:, unstriped(offs4)] = np.tile(f64(wg2), (H // 128, 1)) * h2
    x = page[:, unstriped(offs5)] - f64(base)[:, None]
    y = mxq(f64(w3), 0, "e4m3").T @ mxq(x, 0, "e4m3")
    b = unpack_weight(w4_words, w4_scales, "e4m3").T @ mxq(f64(plan), 0, "e4m3")
    return y * (1.0 / (1.0 + np.exp(-b)))

@@ -1,0 +1,370 @@
+import math
+from contextlib import ExitStack
+
+import concourse.mybir as mybir
+from concourse.masks import make_identity
+
+K, M, H, N, T, S, T2, P_OUT = 1024, 512, 1024, 512, 2048, 512, 2048, 1024
+FLOPS = 2 * (K * H * S + M * H * S + H * N * P_OUT + M * N * P_OUT)
+
+F32 = mybir.dt.float32
+BF16 = mybir.dt.bfloat16
+I32 = mybir.dt.int32
+U32 = mybir.dt.uint32
+U16 = mybir.dt.uint16
+U8 = mybir.dt.uint8
+FP8X4 = mybir.dt.float8_e4m3fn_x4
+FP4X4 = mybir.dt.float4_e2m1fn_x4
+ACT = mybir.ActivationFunctionType
+ALU = mybir.AluOpType
+
+P = 128
+PACK = 4
+PASS = P * PACK
+HALF = 512
+QUARTER = 256
+ROUNDER = 1.5 * 2.0**23
+
+
+def tile_list_cavern_creep_page_kernel(
+    tc, tab_words, tab_scales, offs, tab2_words, tab2_scales, offs2, w1, gain, w2_words, w2_scales,
+    page0, wg1, wg2, offs3, offs4, offs5, base, w3, plan, w4_words, w4_scales, out,
+):
+    nc = tc.nc
+    with ExitStack() as ctx:
+        sb = ctx.enter_context(tc.tile_pool(name="sb", bufs=1))
+        ps = ctx.enter_context(tc.psum_pool(name="ps", bufs=1))
+
+        def held(name, width, dtype, tag=""):
+            return sb.tile([P, width], dtype, name=name, tag=tag or name, align_bytes=64)
+
+        def cols(start, width):
+            return slice(start, start + width)
+
+        list1 = sb.tile([P, S // 16], U16, name="list1")
+        list2 = sb.tile([P, S // 16], U16, name="list2")
+        list3 = sb.tile([P, S // 16], U16, name="list3")
+        list4 = sb.tile([P, S // 16], U16, name="list4")
+        list5 = sb.tile([P, P_OUT // 16], U16, name="list5")
+
+        banks_a = [ps.tile([P, HALF], F32, name="bank_a%d" % i) for i in range(4)]
+        banks_b = [ps.tile([P, HALF], F32, name="bank_b%d" % i) for i in range(4)]
+
+        pages = [held("page%d" % u, T2, F32) for u in range(8)]
+        v2_table = held("v2_table", T, U32, "shared0")
+        v_table = [held("v_table%d" % a, T, U32, "shared%d" % (a + 1)) for a in range(2)]
+        v2_table_scales = held("v2_table_scales", T, U8)
+        v_table_scales = held("v_table_scales", T, U8)
+        v2_codes = held("v2_codes", S, U32)
+        v2_scales = held("v2_scales", S, U8)
+        v_codes = [held("v_codes%d" % a, S, U32) for a in range(2)]
+        v_scales = held("v_scales", S, U8)
+        w2_raw = held("w2_raw", 2 * H, U8)
+        w2_raw_scales = held("w2_raw_scales", H, U8)
+        w2_codes = held("w2_codes", 2 * H, U8)
+        w2_dealt_scales = held("w2_dealt_scales", H, U8)
+        w4_codes = held("w4_codes", N, U32)
+        w4_plane = held("w4_plane", N, U8)
+        wg1_sb = held("wg1_sb", PACK * S, F32)
+        wg2_sb = held("wg2_sb", PACK * S, F32)
+        gain_sb = held("gain_sb", 8, F32)
+        base_sb = held("base_sb", 8, F32)
+        base_wide = held("base_wide", 8 * HALF, F32)
+        ident = held("ident", P, F32)
+        warm = held("warm", 1, F32)
+        raw0 = held("raw0", PACK * HALF, F32)
+        raw1 = held("raw1", PACK * HALF, F32)
+        stage = [held("stage%d" % i, PACK * HALF, BF16) for i in range(2)]
+        moving = [(held("moving_codes%d" % i, HALF, U32), held("moving_scales%d" % i, HALF, U8)) for i in range(4)]
+        w3_q = [(held("w3_codes%d" % i, N, U32), held("w3_scales%d" % i, N, U8)) for i in range(2)]
+        plan_q = [(held("plan_codes%d" % i, HALF, U32), held("plan_scales%d" % i, HALF, U8)) for i in range(2)]
+        h_sb = held("h_sb", 8 * S, F32)
+        turns = held("turns", PACK * S, F32)
+        whole = held("whole", PACK * S, F32)
+        rounded = [held("rounded%d" % i, HALF, U32) for i in range(2)]
+
+        def load(dst, src):
+            nc.sync.dma_start(out=dst, in_=src)
+
+        def load_words(dst, words):
+            load(dst[:].bitcast(I32), words.rearrange("p t i -> p (t i)").bitcast(I32))
+
+        def load_plane(dst, scales):
+            passes = scales.shape[0]
+            for q in range(4):
+                load(dst[32 * q : 32 * q + 4 * passes, :].bitcast(I32), scales[:, 4 * q : 4 * q + 4, :].bitcast(I32))
+
+        def load_full_plane(dst, scales):
+            for q in (0, 2, 1, 3):
+                rows = scales[0, 4 * q : 4 * q + 4, :].bitcast(I32)
+                load(dst[32 * q : 32 * q + 32, :].bitcast(I32), rows.partition_broadcast(8))
+
+        def load_page(u):
+            b, t = divmod(u, PACK)
+            load(pages[u][:], page0[cols(PASS * b, PASS), :].rearrange("(p t) c -> p t c", t=PACK)[:, t, :])
+
+        def load_dealt(dst, wg, t0, count):
+            part = cols(t0 * S, count * S)
+            for q in (0, 2, 1, 3):
+                load(dst[32 * q : 32 * q + 32, part], wg.rearrange("(p t) j -> p (t j)", t=PACK)[:, part])
+
+        def load_vector(dst, vec):
+            load(dst[:].rearrange("p (b t) -> p b t", t=PACK), vec.rearrange("(b p t) -> p b t", p=P, t=PACK))
+
+        def load_rows(dst, matrix, row0, col0):
+            src = matrix[cols(row0, PASS), cols(col0, HALF)].rearrange("(p t) c -> p t c", t=PACK)
+            load(dst[:].rearrange("p (t c) -> p t c", t=PACK), src)
+
+        def weave(dst, src, parts):
+            src4 = src.rearrange("p (t c i) -> p c t i", t=PACK, i=4)
+            dst4 = dst.rearrange("p (c i t) -> p c t i", t=PACK, i=4)
+            step = src4.shape[1] // parts
+            for part in range(parts):
+                nc.scalar.copy(out=dst4[:, cols(part * step, step)], in_=src4[:, cols(part * step, step)])
+
+        def quantize(codes, scales, woven):
+            nc.vector.quantize_mx(out=codes.bitcast(FP8X4), scales=scales, in_=woven)
+
+        def h_slot(u):
+            return h_sb[:, cols(u * S, S)]
+
+        def scatter(u, offsets, wg_sb):
+            t = u % PACK
+            nc.vector.tensor_tensor(pages[u][:].indirect(offsets[:]), h_slot(u), wg_sb[:, cols(t * S, S)], ALU.mult)
+
+        def fetch(u, dst, j0, width):
+            window = pages[u][:].indirect(list5[:, cols(j0 // 16, width // 16)])
+            nc.vector.tensor_tensor(dst, window, base_wide[:, cols(u * HALF, width)], ALU.subtract)
+
+        nc.vector.memset(v_table_scales[:].bitcast(I32), 0)
+        nc.vector.memset(w4_plane[:].bitcast(I32), 0)
+        make_identity(nc, ident[:])
+        nc.scalar.activation(out=warm[:], in_=ident[:, 0:1], func=ACT.Sqrt)
+
+        load(list2[:], offs2)
+        load_full_plane(v2_table_scales, tab2_scales)
+        load(w2_raw[:].bitcast(I32), w2_words[0].bitcast(I32))
+        load_words(v2_table, tab2_words[0])
+        load_full_plane(w2_raw_scales, w2_scales)
+        load_page(0)
+        load(list4[:], offs4)
+        load_dealt(wg2_sb, wg2, 0, 1)
+
+        nc.vector.tensor_copy(out=v2_scales[:], in_=v2_table_scales[:].indirect(list2[:]))
+        nc.vector.tensor_copy(
+            out=w2_codes[:].bitcast(U16).rearrange("p (b t m) -> p b t m", b=2, t=PACK),
+            in_=w2_raw[:].bitcast(U16).rearrange("p (b m t) -> p b t m", b=2, t=PACK),
+        )
+        nc.vector.tensor_copy(out=v2_codes[:], in_=v2_table[:].indirect(list2[:]))
+        for slots in (slice(0, 1), slice(1, PACK)):
+            nc.vector.tensor_copy(
+                out=w2_dealt_scales[:].rearrange("p (b t m) -> p b t m", b=2, t=PACK)[:, :, slots, :],
+                in_=w2_raw_scales[:].rearrange("p (b m t) -> p b t m", b=2, t=PACK)[:, :, slots, :],
+            )
+
+        by_slot = [PACK * b + t for t in range(PACK) for b in range(2)]
+        for i, u in enumerate(by_slot):
+            bank = banks_a[i % 4]
+            nc.tensor.matmul_mx(
+                out=bank[:],
+                lhsT=w2_codes[:, cols(2 * P * u, 2 * P)].bitcast(FP4X4),
+                lhsT_scale=w2_dealt_scales[:, cols(P * u, P)],
+                rhs=v2_codes[:].bitcast(FP8X4),
+                rhs_scale=v2_scales[:],
+                start=True,
+                stop=True,
+            )
+            nc.scalar.activation(out=h_slot(u), in_=bank[:], func=ACT.Abs)
+            nc.scalar.activation(out=h_slot(u), in_=h_slot(u), func=ACT.Sqrt)
+
+        raw2 = held("raw2", PACK * HALF, F32, "shared0")
+
+        load_page(4)
+        load_dealt(wg2_sb, wg2, 1, 3)
+        load_page(1)
+        load_vector(base_sb, base)
+        load_page(5)
+        load_rows(raw0, w1, 0, 0)
+        load(list1[:], offs)
+        load_plane(v_table_scales, tab_scales)
+        load_words(v_table[0], tab_words[0])
+        load_page(2)
+        load_rows(raw1, w1, PASS, 0)
+        load_words(v_table[1], tab_words[1])
+        load_page(6)
+        load_vector(gain_sb, gain)
+        load_page(3)
+        load_page(7)
+        load(list3[:], offs3)
+        load(list5[:], offs5)
+        load_dealt(wg1_sb, wg1, 0, 2)
+        load_rows(raw2, w1, 0, HALF)
+
+        for u in by_slot[:4]:
+            scatter(u, list4, wg2_sb)
+        weave(stage[0][:], raw0[:], 2)
+        for u in range(8):
+            nc.scalar.copy(out=base_wide[:, cols(u * HALF, HALF)], in_=base_sb[:, u : u + 1].to_broadcast([P, HALF]))
+        nc.vector.tensor_copy(out=v_scales[:], in_=v_table_scales[:].indirect(list1[:]))
+        nc.vector.tensor_copy(out=v_codes[0][:], in_=v_table[0][:].indirect(list1[:]))
+        quantize(moving[0][0][:], moving[0][1][:], stage[0][:])
+        scatter(by_slot[4], list4, wg2_sb)
+        weave(stage[1][:], raw1[:], 2)
+        nc.vector.tensor_copy(out=v_codes[1][:], in_=v_table[1][:].indirect(list1[:]))
+        quantize(moving[1][0][:], moving[1][1][:], stage[1][:])
+        for u in by_slot[5:]:
+            scatter(u, list4, wg2_sb)
+
+        load_rows(raw0, w1, PASS, HALF)
+        load_rows(raw1, plan, 0, 0)
+
+        turns4 = turns[:].rearrange("j (t g p) -> j t g p", t=PACK, g=4)
+        whole4 = whole[:].rearrange("j (t g p) -> j t g p", t=PACK, g=4)
+
+        def to_turns(g, slots):
+            nc.scalar.activation(
+                out=turns4[:, slots, g, :], in_=banks_a[g][:].rearrange("j (p t) -> j t p", t=PACK)[:, slots, :],
+                func=ACT.Copy, scale=1.0 / (2.0 * math.pi),
+            )
+
+        def sine(u):
+            t = u % PACK
+            part = cols(t * S, S)
+            count = rounded[t % 2]
+            nc.scalar.activation(out=count[:], in_=turns[:, part], func=ACT.Copy, bias=ROUNDER)
+            nc.scalar.activation(out=whole[:, part], in_=count[:], func=ACT.Copy, scale=-1.0, bias=ROUNDER)
+            for g in range(4):
+                for src, first in ((turns4, True), (whole4, False)):
+                    nc.tensor.matmul(
+                        out=banks_b[t][:, cols(P * g, P)], lhsT=src[:, t, g, :], rhs=ident[:],
+                        start=first, stop=not first, is_transpose=True,
+                    )
+            nc.scalar.activation(out=whole[:, part], in_=banks_b[t][:], func=ACT.Sin, scale=2.0 * math.pi)
+            nc.scalar.activation(out=h_slot(u), in_=whole[:, part], func=ACT.Copy, scale=gain_sb[:, u : u + 1])
+
+        def sines(b):
+            for g in range(4):
+                for a in range(2):
+                    codes, scales = moving[2 * b + a]
+                    nc.tensor.matmul_mx(
+                        out=banks_a[g][:],
+                        lhsT=v_codes[a][:, cols(P * g, P)].bitcast(FP8X4),
+                        lhsT_scale=v_scales[4 * a : P, cols(P * g, P)],
+                        rhs=codes[:].bitcast(FP8X4),
+                        rhs_scale=scales[:],
+                        start=(a == 0),
+                        stop=(a == 1),
+                    )
+                to_turns(g, slice(0, 1))
+            sine(PACK * b)
+            for g in range(4):
+                to_turns(g, slice(1, PACK))
+            for t in range(1, PACK):
+                sine(PACK * b + t)
+
+        sines(0)
+        for i, raw in enumerate((raw2, raw0)):
+            weave(stage[i][:], raw[:], 2)
+            quantize(moving[2 + i][0][:], moving[2 + i][1][:], stage[i][:])
+
+        load_rows(raw2, plan, 0, HALF)
+        load_dealt(wg1_sb, wg1, 2, 2)
+        load_words(w4_codes, w4_words[0])
+        load_plane(w4_plane, w4_scales)
+        load_rows(raw0, w3, 0, 0)
+
+        x_first = [held("x_first%d" % i, PACK * HALF, F32, "shared%d" % (i + 1)) for i in range(2)]
+        for u in range(4):
+            scatter(u, list3, wg1_sb)
+            for half in range(2):
+                fetch(u, x_first[half][:, cols(u * HALF, HALF)], half * HALF, HALF)
+
+        for half, raw in enumerate((raw1, raw2)):
+            weave(stage[half][:], raw[:], 2)
+            quantize(plan_q[half][0][:], plan_q[half][1][:], stage[half][:])
+        load_rows(raw1, w3, PASS, 0)
+        sines(1)
+        for u in range(4, 8):
+            scatter(u, list3, wg1_sb)
+        for b, raw in enumerate((raw0, raw1)):
+            weave(stage[b][:], raw[:], 2)
+            quantize(w3_q[b][0][:], w3_q[b][1][:], stage[b][:])
+
+        woven_first = [whole[:, cols(half * 2 * S, 2 * S)].bitcast(BF16) for half in range(2)]
+        for half in range(2):
+            weave(woven_first[half], x_first[half][:], 1)
+
+        gates = [turns, raw2]
+        for half in range(2):
+            for n in range(4):
+                nc.tensor.matmul_mx(
+                    out=banks_b[n][:],
+                    lhsT=w4_codes[:, cols(P * n, P)].bitcast(FP8X4),
+                    lhsT_scale=w4_plane[:, cols(P * n, P)],
+                    rhs=plan_q[half][0][:].bitcast(FP8X4),
+                    rhs_scale=plan_q[half][1][:],
+                    start=True,
+                    stop=True,
+                )
+                nc.scalar.activation(out=gates[half][:, cols(n * HALF, HALF)], in_=banks_b[n][:], func=ACT.Sigmoid)
+
+        def score_pass(dst, n, b, codes, scales):
+            nc.tensor.matmul_mx(
+                out=dst,
+                lhsT=w3_q[b][0][:, cols(P * n, P)].bitcast(FP8X4),
+                lhsT_scale=w3_q[b][1][:, cols(P * n, P)],
+                rhs=codes.bitcast(FP8X4),
+                rhs_scale=scales,
+                start=(b == 0),
+                stop=(b == 1),
+            )
+
+        x_third = x_first[0][:, cols(0, PACK * QUARTER)]
+        x_fourth = x_first[1][:, cols(0, PACK * QUARTER)]
+        woven_third = x_first[1][:, cols(QUARTER // 2, 2 * QUARTER)].bitcast(BF16)
+        woven_fourth = stage[1][:, cols(0, PACK * QUARTER)]
+
+        quantize(moving[0][0][:], moving[0][1][:], woven_first[0])
+        for t in range(PACK):
+            fetch(4 + t, x_third[:, cols(t * QUARTER, QUARTER)], HALF, QUARTER)
+        quantize(moving[1][0][:], moving[1][1][:], woven_first[1])
+        for t in range(PACK):
+            fetch(4 + t, whole[:, cols(t * HALF, HALF)], 0, HALF)
+        for n in range(4):
+            score_pass(banks_b[n][:], n, 0, moving[0][0][:], moving[0][1][:])
+
+        def quarter(i, woven):
+            part = cols(i * QUARTER, QUARTER)
+            quantize(moving[3][0][:, part], moving[3][1][:, part], woven)
+            for n in range(4):
+                dst = banks_a[2 * i + n // 2][:, cols((n % 2) * QUARTER, QUARTER)]
+                score_pass(dst, n, 0, moving[1][0][:, part], moving[1][1][:, part])
+                score_pass(dst, n, 1, moving[3][0][:, part], moving[3][1][:, part])
+
+        def finish_quarter(i):
+            gate = gates[1][:].rearrange("p (n c) -> p n c", n=4)
+            for pair in range(2):
+                slot = 2 * i + pair
+                result = h_slot(4 + slot).rearrange("p (n c) -> p n c", n=2)
+                nc.vector.tensor_tensor(
+                    result, banks_a[slot][:].rearrange("p (n c) -> p n c", n=2),
+                    gate[:, cols(2 * pair, 2), cols(i * QUARTER, QUARTER)], ALU.mult,
+                )
+                dst = out[cols(2 * P * pair, 2 * P), cols(HALF + i * QUARTER, QUARTER)]
+                nc.sync.dma_start(out=dst.rearrange("(n p) c -> p n c", p=P), in_=result)
+
+        weave(woven_third, x_third, 1)
+        quarter(0, woven_third)
+        weave(stage[0][:], whole[:], 1)
+        for t in range(PACK):
+            fetch(4 + t, x_fourth[:, cols(t * QUARTER, QUARTER)], HALF + QUARTER, QUARTER)
+        quantize(moving[2][0][:], moving[2][1][:], stage[0][:])
+        for n in range(4):
+            score_pass(banks_b[n][:], n, 1, moving[2][0][:], moving[2][1][:])
+        finish_quarter(0)
+        weave(woven_fourth, x_fourth, 1)
+        quarter(1, woven_fourth)
+        for n in range(4):
+            nc.vector.tensor_tensor(h_slot(n), banks_b[n][:], gates[0][:, cols(n * HALF, HALF)], ALU.mult)
+            nc.sync.dma_start(out=out[cols(P * n, P), cols(0, HALF)], in_=h_slot(n))
+        finish_quarter(1)

@@ -116,8 +116,8 @@ def tile_list_cavern_creep_page_kernel(
             load(dst[:].rearrange("p (t c) -> p t c", t=PACK), src)
 
         def weave(dst, src, parts):
-            src4 = src.rearrange("p (t c i) -> p c t i", t=PACK, i=4)
-            dst4 = dst.rearrange("p (c i t) -> p c t i", t=PACK, i=4)
+            src4 = src.rearrange("p (t c) -> p c t", t=PACK)
+            dst4 = dst.rearrange("p (c t) -> p c t", t=PACK)
             step = src4.shape[1] // parts
             for part in range(parts):
                 nc.scalar.copy(out=dst4[:, cols(part * step, step)], in_=src4[:, cols(part * step, step)])

@@ -94,19 +94,9 @@ def tile_list_cavern_creep_page_kernel(
             for q in range(4):
                 load(dst[32 * q : 32 * q + 4 * passes, :].bitcast(I32), scales[:, 4 * q : 4 * q + 4, :].bitcast(I32))
 
-        def load_full_plane(dst, scales):
-            for q in (0, 2, 1, 3):
-                rows = scales[0, 4 * q : 4 * q + 4, :].bitcast(I32)
-                load(dst[32 * q : 32 * q + 32, :].bitcast(I32), rows.partition_broadcast(8))
-
         def load_page(u):
             b, t = divmod(u, PACK)
             load(pages[u][:], page0[cols(PASS * b, PASS), :].rearrange("(p t) c -> p t c", t=PACK)[:, t, :])
-
-        def load_dealt(dst, wg, t0, count):
-            part = cols(t0 * S, count * S)
-            for q in (0, 2, 1, 3):
-                load(dst[32 * q : 32 * q + 32, part], wg.rearrange("(p t) j -> p (t j)", t=PACK)[:, part])
 
         def load_vector(dst, vec):
             load(dst[:].rearrange("p (b t) -> p b t", t=PACK), vec.rearrange("(b p t) -> p b t", p=P, t=PACK))
@@ -116,8 +106,8 @@ def tile_list_cavern_creep_page_kernel(
             load(dst[:].rearrange("p (t c) -> p t c", t=PACK), src)
 
         def weave(dst, src, parts):
-            src4 = src.rearrange("p (t c) -> p c t", t=PACK)
-            dst4 = dst.rearrange("p (c t) -> p c t", t=PACK)
+            src4 = src.rearrange("p (t c i) -> p c t i", t=PACK, i=4)
+            dst4 = dst.rearrange("p (c i t) -> p c t i", t=PACK, i=4)
             step = src4.shape[1] // parts
             for part in range(parts):
                 nc.scalar.copy(out=dst4[:, cols(part * step, step)], in_=src4[:, cols(part * step, step)])
@@ -136,19 +126,38 @@ def tile_list_cavern_creep_page_kernel(
             window = pages[u][:].indirect(list5[:, cols(j0 // 16, width // 16)])
             nc.vector.tensor_tensor(dst, window, base_wide[:, cols(u * HALF, width)], ALU.subtract)
 
+        turns4 = turns[:].rearrange("j (t g p) -> j t g p", t=PACK, g=4)
+        whole4 = whole[:].rearrange("j (t g p) -> j t g p", t=PACK, g=4)
+
+        def turn(natural):
+            for g in range(4):
+                nc.tensor.transpose(banks_b[3][:, cols(P * g, P)], natural[:, cols(P * g, P)], ident[:])
+
+        def repeat(t0, count):
+            src = banks_b[3][:].rearrange("j (g m t) -> j t g m", g=4, t=PACK)[:, cols(t0, count)]
+            dst = turns[:].rearrange("j (t g q m) -> j t g q m", t=PACK, g=4, q=4)[:, cols(t0, count)]
+            nc.scalar.copy(out=dst, in_=src.unsqueeze(3).to_broadcast([P, count, 4, 4, 32]))
+
+        def turn_back(dealt, t):
+            for g in range(4):
+                nc.tensor.transpose(banks_b[t][:, cols(P * g, P)], turns4[:, t, g, :], ident[:])
+            nc.scalar.copy(out=dealt[:, cols(t * S, S)], in_=banks_b[t][:])
+
+        nc.gpsimd.memset(v2_table_scales[:].bitcast(I32), 0)
+        nc.gpsimd.memset(w2_raw_scales[:].bitcast(I32), 0)
         nc.vector.memset(v_table_scales[:].bitcast(I32), 0)
         nc.vector.memset(w4_plane[:].bitcast(I32), 0)
         make_identity(nc, ident[:])
         nc.scalar.activation(out=warm[:], in_=ident[:, 0:1], func=ACT.Sqrt)
 
         load(list2[:], offs2)
-        load_full_plane(v2_table_scales, tab2_scales)
         load(w2_raw[:].bitcast(I32), w2_words[0].bitcast(I32))
+        load_plane(v2_table_scales, tab2_scales)
+        load(whole[:, cols(0, S)], wg2)
         load_words(v2_table, tab2_words[0])
-        load_full_plane(w2_raw_scales, w2_scales)
+        load_plane(w2_raw_scales, w2_scales)
         load_page(0)
         load(list4[:], offs4)
-        load_dealt(wg2_sb, wg2, 0, 1)
 
         nc.vector.tensor_copy(out=v2_scales[:], in_=v2_table_scales[:].indirect(list2[:]))
         nc.vector.tensor_copy(
@@ -163,7 +172,9 @@ def tile_list_cavern_creep_page_kernel(
             )
 
         by_slot = [PACK * b + t for t in range(PACK) for b in range(2)]
-        for i, u in enumerate(by_slot):
+
+        def root(i):
+            u = by_slot[i]
             bank = banks_a[i % 4]
             nc.tensor.matmul_mx(
                 out=bank[:],
@@ -177,10 +188,20 @@ def tile_list_cavern_creep_page_kernel(
             nc.scalar.activation(out=h_slot(u), in_=bank[:], func=ACT.Abs)
             nc.scalar.activation(out=h_slot(u), in_=h_slot(u), func=ACT.Sqrt)
 
+        turn(whole[:, cols(0, S)])
+        repeat(0, 1)
+        turn_back(wg2_sb, 0)
+        for i in range(2):
+            root(i)
+        repeat(1, PACK - 1)
+        for t in range(1, PACK):
+            turn_back(wg2_sb, t)
+        for i in range(2, 8):
+            root(i)
+
         raw2 = held("raw2", PACK * HALF, F32, "shared0")
 
         load_page(4)
-        load_dealt(wg2_sb, wg2, 1, 3)
         load_page(1)
         load_vector(base_sb, base)
         load_page(5)
@@ -188,38 +209,37 @@ def tile_list_cavern_creep_page_kernel(
         load(list1[:], offs)
         load_plane(v_table_scales, tab_scales)
         load_words(v_table[0], tab_words[0])
-        load_page(2)
         load_rows(raw1, w1, PASS, 0)
         load_words(v_table[1], tab_words[1])
+        load(whole[:, cols(S, S)], wg1)
+        load_page(2)
         load_page(6)
         load_vector(gain_sb, gain)
         load_page(3)
         load_page(7)
         load(list3[:], offs3)
         load(list5[:], offs5)
-        load_dealt(wg1_sb, wg1, 0, 2)
         load_rows(raw2, w1, 0, HALF)
 
         for u in by_slot[:4]:
             scatter(u, list4, wg2_sb)
         weave(stage[0][:], raw0[:], 2)
-        for u in range(8):
-            nc.scalar.copy(out=base_wide[:, cols(u * HALF, HALF)], in_=base_sb[:, u : u + 1].to_broadcast([P, HALF]))
+        weave(stage[1][:], raw1[:], 2)
+        turn(whole[:, cols(S, S)])
+        for t in range(PACK):
+            repeat(t, 1)
+        for t in range(PACK):
+            turn_back(wg1_sb, t)
         nc.vector.tensor_copy(out=v_scales[:], in_=v_table_scales[:].indirect(list1[:]))
         nc.vector.tensor_copy(out=v_codes[0][:], in_=v_table[0][:].indirect(list1[:]))
         quantize(moving[0][0][:], moving[0][1][:], stage[0][:])
-        scatter(by_slot[4], list4, wg2_sb)
-        weave(stage[1][:], raw1[:], 2)
         nc.vector.tensor_copy(out=v_codes[1][:], in_=v_table[1][:].indirect(list1[:]))
         quantize(moving[1][0][:], moving[1][1][:], stage[1][:])
-        for u in by_slot[5:]:
+        for u in by_slot[4:]:
             scatter(u, list4, wg2_sb)
 
         load_rows(raw0, w1, PASS, HALF)
         load_rows(raw1, plan, 0, 0)
-
-        turns4 = turns[:].rearrange("j (t g p) -> j t g p", t=PACK, g=4)
-        whole4 = whole[:].rearrange("j (t g p) -> j t g p", t=PACK, g=4)
 
         def to_turns(g, slots):
             nc.scalar.activation(
@@ -259,16 +279,23 @@ def tile_list_cavern_creep_page_kernel(
             sine(PACK * b)
             for g in range(4):
                 to_turns(g, slice(1, PACK))
-            for t in range(1, PACK):
-                sine(PACK * b + t)
+            sine(PACK * b + 1)
+
+        def widen(u):
+            nc.scalar.copy(out=base_wide[:, cols(u * HALF, HALF)], in_=base_sb[:, u : u + 1].to_broadcast([P, HALF]))
 
         sines(0)
+        for u in range(2):
+            widen(u)
         for i, raw in enumerate((raw2, raw0)):
             weave(stage[i][:], raw[:], 2)
             quantize(moving[2 + i][0][:], moving[2 + i][1][:], stage[i][:])
+        for u in range(2, 4):
+            sine(u)
+        for u in range(2, 8):
+            widen(u)
 
         load_rows(raw2, plan, 0, HALF)
-        load_dealt(wg1_sb, wg1, 2, 2)
         load_words(w4_codes, w4_words[0])
         load_plane(w4_plane, w4_scales)
         load_rows(raw0, w3, 0, 0)
@@ -284,6 +311,8 @@ def tile_list_cavern_creep_page_kernel(
             quantize(plan_q[half][0][:], plan_q[half][1][:], stage[half][:])
         load_rows(raw1, w3, PASS, 0)
         sines(1)
+        for u in range(6, 8):
+            sine(u)
         for u in range(4, 8):
             scatter(u, list3, wg1_sb)
         for b, raw in enumerate((raw0, raw1)):

@@ -4,8 +4,8 @@ from contextlib import ExitStack
 import concourse.mybir as mybir
 from concourse.masks import make_identity
 
-K, M, H, N, T, S, T2, P_OUT = 1024, 512, 1024, 512, 2048, 512, 2048, 1024
-FLOPS = 2 * (K * H * S + M * H * S + H * N * P_OUT + M * N * P_OUT)
+K, M, H, N, T, S, T2, J = 1024, 512, 1024, 512, 2048, 512, 2048, 1024
+FLOPS = 2 * (K * H * S + M * H * S + H * N * J + M * N * J)
 
 F32 = mybir.dt.float32
 BF16 = mybir.dt.bfloat16
@@ -21,8 +21,11 @@ ALU = mybir.AluOpType
 P = 128
 PACK = 4
 PASS = P * PACK
-HALF = 512
-QUARTER = 256
+TILES = H // P
+BANK = 512
+HALF_BANK = 256
+GROUPS = BANK // P
+QUADRANT = 32
 ROUNDER = 1.5 * 2.0**23
 
 
@@ -45,12 +48,12 @@ def tile_list_cavern_creep_page_kernel(
         list2 = sb.tile([P, S // 16], U16, name="list2")
         list3 = sb.tile([P, S // 16], U16, name="list3")
         list4 = sb.tile([P, S // 16], U16, name="list4")
-        list5 = sb.tile([P, P_OUT // 16], U16, name="list5")
+        list5 = sb.tile([P, J // 16], U16, name="list5")
 
-        banks_a = [ps.tile([P, HALF], F32, name="bank_a%d" % i) for i in range(4)]
-        banks_b = [ps.tile([P, HALF], F32, name="bank_b%d" % i) for i in range(4)]
+        banks_a = [ps.tile([P, BANK], F32, name="bank_a%d" % i) for i in range(4)]
+        banks_b = [ps.tile([P, BANK], F32, name="bank_b%d" % i) for i in range(4)]
 
-        pages = [held("page%d" % u, T2, F32) for u in range(8)]
+        pages = [held("page%d" % u, T2, F32) for u in range(TILES)]
         v2_table = held("v2_table", T, U32, "shared0")
         v_table = [held("v_table%d" % a, T, U32, "shared%d" % (a + 1)) for a in range(2)]
         v2_table_scales = held("v2_table_scales", T, U8)
@@ -65,23 +68,24 @@ def tile_list_cavern_creep_page_kernel(
         w2_dealt_scales = held("w2_dealt_scales", H, U8)
         w4_codes = held("w4_codes", N, U32)
         w4_plane = held("w4_plane", N, U8)
-        wg1_sb = held("wg1_sb", PACK * S, F32)
-        wg2_sb = held("wg2_sb", PACK * S, F32)
-        gain_sb = held("gain_sb", 8, F32)
-        base_sb = held("base_sb", 8, F32)
-        base_wide = held("base_wide", 8 * HALF, F32)
+        wg1_gain = held("wg1_gain", TILES * S, F32)
+        wg2_dealt = held("wg2_dealt", PACK * S, F32)
+        gain_sb = held("gain_sb", TILES, F32)
+        base_sb = held("base_sb", TILES, F32)
+        base_wide = held("base_wide", TILES * BANK, F32)
         ident = held("ident", P, F32)
         warm = held("warm", 1, F32)
-        raw0 = held("raw0", PACK * HALF, F32)
-        raw1 = held("raw1", PACK * HALF, F32)
-        stage = [held("stage%d" % i, PACK * HALF, BF16) for i in range(2)]
-        moving = [(held("moving_codes%d" % i, HALF, U32), held("moving_scales%d" % i, HALF, U8)) for i in range(4)]
+        raw0 = held("raw0", PACK * BANK, F32)
+        raw1 = held("raw1", PACK * BANK, F32)
+        stage = [held("stage%d" % i, PACK * BANK, BF16) for i in range(2)]
+        moving = [(held("moving_codes%d" % i, BANK, U32), held("moving_scales%d" % i, BANK, U8)) for i in range(4)]
         w3_q = [(held("w3_codes%d" % i, N, U32), held("w3_scales%d" % i, N, U8)) for i in range(2)]
-        plan_q = [(held("plan_codes%d" % i, HALF, U32), held("plan_scales%d" % i, HALF, U8)) for i in range(2)]
-        h_sb = held("h_sb", 8 * S, F32)
+        plan_q = [(held("plan_codes%d" % i, BANK, U32), held("plan_scales%d" % i, BANK, U8)) for i in range(2)]
+        h_sb = held("h_sb", TILES * S, F32)
         turns = held("turns", PACK * S, F32)
-        whole = held("whole", PACK * S, F32)
-        rounded = [held("rounded%d" % i, HALF, U32) for i in range(2)]
+        repeated = held("repeated", PACK * S, F32)
+        spare = held("spare", PACK * S, F32)
+        rounded = [held("rounded%d" % i, S, U32) for i in range(2)]
 
         def load(dst, src):
             nc.sync.dma_start(out=dst, in_=src)
@@ -92,7 +96,8 @@ def tile_list_cavern_creep_page_kernel(
         def load_plane(dst, scales):
             passes = scales.shape[0]
             for q in range(4):
-                load(dst[32 * q : 32 * q + 4 * passes, :].bitcast(I32), scales[:, 4 * q : 4 * q + 4, :].bitcast(I32))
+                rows = cols(QUADRANT * q, 4 * passes)
+                load(dst[rows, :].bitcast(I32), scales[:, cols(4 * q, 4), :].bitcast(I32))
 
         def load_page(u):
             b, t = divmod(u, PACK)
@@ -102,7 +107,7 @@ def tile_list_cavern_creep_page_kernel(
             load(dst[:].rearrange("p (b t) -> p b t", t=PACK), vec.rearrange("(b p t) -> p b t", p=P, t=PACK))
 
         def load_rows(dst, matrix, row0, col0):
-            src = matrix[cols(row0, PASS), cols(col0, HALF)].rearrange("(p t) c -> p t c", t=PACK)
+            src = matrix[cols(row0, PASS), cols(col0, BANK)].rearrange("(p t) c -> p t c", t=PACK)
             load(dst[:].rearrange("p (t c) -> p t c", t=PACK), src)
 
         def weave(dst, src, parts):
@@ -115,33 +120,41 @@ def tile_list_cavern_creep_page_kernel(
         def quantize(codes, scales, woven):
             nc.vector.quantize_mx(out=codes.bitcast(FP8X4), scales=scales, in_=woven)
 
+        def entries(offsets, j0, width):
+            return offsets[:, cols(j0 // 16, width // 16)]
+
         def h_slot(u):
             return h_sb[:, cols(u * S, S)]
 
-        def scatter(u, offsets, wg_sb):
-            t = u % PACK
-            nc.vector.tensor_tensor(pages[u][:].indirect(offsets[:]), h_slot(u), wg_sb[:, cols(t * S, S)], ALU.mult)
+        def put(u, offsets, factors, j0, width):
+            part = cols(j0, width)
+            window = pages[u][:].indirect(entries(offsets, j0, width))
+            nc.vector.tensor_tensor(window, h_slot(u)[:, part], factors[:, part], ALU.mult)
+
+        def put_h2(u, j0=0, width=S):
+            put(u, list4, wg2_dealt[:, cols(u % PACK * S, S)], j0, width)
+
+        def put_h1(u):
+            put(u, list3, wg1_gain[:, cols(u * S, S)], 0, S)
 
         def fetch(u, dst, j0, width):
-            window = pages[u][:].indirect(list5[:, cols(j0 // 16, width // 16)])
-            nc.vector.tensor_tensor(dst, window, base_wide[:, cols(u * HALF, width)], ALU.subtract)
-
-        turns4 = turns[:].rearrange("j (t g p) -> j t g p", t=PACK, g=4)
-        whole4 = whole[:].rearrange("j (t g p) -> j t g p", t=PACK, g=4)
+            window = pages[u][:].indirect(entries(list5, j0, width))
+            nc.vector.tensor_tensor(dst, window, base_wide[:, cols(u * BANK, width)], ALU.subtract)
 
         def turn(natural):
-            for g in range(4):
+            for g in range(GROUPS):
                 nc.tensor.transpose(banks_b[3][:, cols(P * g, P)], natural[:, cols(P * g, P)], ident[:])
 
         def repeat(t0, count):
-            src = banks_b[3][:].rearrange("j (g m t) -> j t g m", g=4, t=PACK)[:, cols(t0, count)]
-            dst = turns[:].rearrange("j (t g q m) -> j t g q m", t=PACK, g=4, q=4)[:, cols(t0, count)]
-            nc.scalar.copy(out=dst, in_=src.unsqueeze(3).to_broadcast([P, count, 4, 4, 32]))
+            src = banks_b[3][:].rearrange("j (g m t) -> j t g m", g=GROUPS, t=PACK)[:, cols(t0, count)]
+            dst = repeated[:].rearrange("j (t g q m) -> j t g q m", t=PACK, g=GROUPS, q=4)[:, cols(t0, count)]
+            nc.scalar.copy(out=dst, in_=src.unsqueeze(3).to_broadcast([P, count, GROUPS, 4, QUADRANT]))
 
-        def turn_back(dealt, t):
-            for g in range(4):
-                nc.tensor.transpose(banks_b[t][:, cols(P * g, P)], turns4[:, t, g, :], ident[:])
-            nc.scalar.copy(out=dealt[:, cols(t * S, S)], in_=banks_b[t][:])
+        def turn_back(t):
+            bank = banks_b[1 + t % 2]
+            for g in range(GROUPS):
+                nc.tensor.transpose(bank[:, cols(P * g, P)], repeated[:, cols(t * S + P * g, P)], ident[:])
+            return bank
 
         nc.gpsimd.memset(v2_table_scales[:].bitcast(I32), 0)
         nc.gpsimd.memset(w2_raw_scales[:].bitcast(I32), 0)
@@ -153,7 +166,7 @@ def tile_list_cavern_creep_page_kernel(
         load(list2[:], offs2)
         load(w2_raw[:].bitcast(I32), w2_words[0].bitcast(I32))
         load_plane(v2_table_scales, tab2_scales)
-        load(whole[:, cols(0, S)], wg2)
+        load(spare[:, cols(0, S)], wg2)
         load_words(v2_table, tab2_words[0])
         load_plane(w2_raw_scales, w2_scales)
         load_page(0)
@@ -164,8 +177,11 @@ def tile_list_cavern_creep_page_kernel(
             out=w2_codes[:].bitcast(U16).rearrange("p (b t m) -> p b t m", b=2, t=PACK),
             in_=w2_raw[:].bitcast(U16).rearrange("p (b m t) -> p b t m", b=2, t=PACK),
         )
-        nc.vector.tensor_copy(out=v2_codes[:], in_=v2_table[:].indirect(list2[:]))
-        for slots in (slice(0, 1), slice(1, PACK)):
+        for half, slots in enumerate((slice(0, 1), slice(1, PACK))):
+            j0 = half * HALF_BANK
+            nc.vector.tensor_copy(
+                out=v2_codes[:, cols(j0, HALF_BANK)], in_=v2_table[:].indirect(entries(list2, j0, HALF_BANK))
+            )
             nc.vector.tensor_copy(
                 out=w2_dealt_scales[:].rearrange("p (b t m) -> p b t m", b=2, t=PACK)[:, :, slots, :],
                 in_=w2_raw_scales[:].rearrange("p (b m t) -> p b t m", b=2, t=PACK)[:, :, slots, :],
@@ -173,73 +189,73 @@ def tile_list_cavern_creep_page_kernel(
 
         by_slot = [PACK * b + t for t in range(PACK) for b in range(2)]
 
-        def root(i):
+        def root(i, j0, width):
             u = by_slot[i]
-            bank = banks_a[i % 4]
+            part = cols(j0, width)
+            bank = banks_a[(i + j0 // width) % 4][:, part]
             nc.tensor.matmul_mx(
-                out=bank[:],
+                out=bank,
                 lhsT=w2_codes[:, cols(2 * P * u, 2 * P)].bitcast(FP4X4),
                 lhsT_scale=w2_dealt_scales[:, cols(P * u, P)],
-                rhs=v2_codes[:].bitcast(FP8X4),
-                rhs_scale=v2_scales[:],
+                rhs=v2_codes[:, part].bitcast(FP8X4),
+                rhs_scale=v2_scales[:, part],
                 start=True,
                 stop=True,
             )
-            nc.scalar.activation(out=h_slot(u), in_=bank[:], func=ACT.Abs)
-            nc.scalar.activation(out=h_slot(u), in_=h_slot(u), func=ACT.Sqrt)
+            nc.scalar.activation(out=h_slot(u)[:, part], in_=bank, func=ACT.Abs)
+            nc.scalar.activation(out=h_slot(u)[:, part], in_=h_slot(u)[:, part], func=ACT.Sqrt)
 
-        turn(whole[:, cols(0, S)])
+        turn(spare[:, cols(0, S)])
         repeat(0, 1)
-        turn_back(wg2_sb, 0)
-        for i in range(2):
-            root(i)
+        nc.scalar.copy(out=wg2_dealt[:, cols(0, S)], in_=turn_back(0)[:])
+        for j0 in (0, HALF_BANK):
+            root(0, j0, HALF_BANK)
+        root(1, 0, S)
         repeat(1, PACK - 1)
         for t in range(1, PACK):
-            turn_back(wg2_sb, t)
-        for i in range(2, 8):
-            root(i)
+            nc.scalar.copy(out=wg2_dealt[:, cols(t * S, S)], in_=turn_back(t)[:])
+        for i in range(2, TILES):
+            root(i, 0, S)
 
-        raw2 = held("raw2", PACK * HALF, F32, "shared0")
+        raw2 = held("raw2", PACK * BANK, F32, "shared0")
 
-        load_page(4)
-        load_page(1)
-        load_vector(base_sb, base)
-        load_page(5)
+        for u in by_slot[1:4]:
+            load_page(u)
         load_rows(raw0, w1, 0, 0)
         load(list1[:], offs)
         load_plane(v_table_scales, tab_scales)
         load_words(v_table[0], tab_words[0])
         load_rows(raw1, w1, PASS, 0)
         load_words(v_table[1], tab_words[1])
-        load(whole[:, cols(S, S)], wg1)
-        load_page(2)
-        load_page(6)
+        wg1_natural = spare[:, cols(3 * S, S)]
+        load(wg1_natural, wg1)
         load_vector(gain_sb, gain)
-        load_page(3)
-        load_page(7)
+        for u in by_slot[4:]:
+            load_page(u)
         load(list3[:], offs3)
         load(list5[:], offs5)
-        load_rows(raw2, w1, 0, HALF)
+        load_vector(base_sb, base)
+        load_rows(raw2, w1, 0, BANK)
 
-        for u in by_slot[:4]:
-            scatter(u, list4, wg2_sb)
+        for j0 in (0, HALF_BANK):
+            put_h2(0, j0, HALF_BANK)
+        for u in by_slot[1:4]:
+            put_h2(u)
         weave(stage[0][:], raw0[:], 2)
         weave(stage[1][:], raw1[:], 2)
-        turn(whole[:, cols(S, S)])
-        for t in range(PACK):
-            repeat(t, 1)
-        for t in range(PACK):
-            turn_back(wg1_sb, t)
+        nc.scalar.activation(out=warm[:], in_=h_slot(by_slot[-1])[:, 0:1], func=ACT.Sin, scale=0.0)
         nc.vector.tensor_copy(out=v_scales[:], in_=v_table_scales[:].indirect(list1[:]))
         nc.vector.tensor_copy(out=v_codes[0][:], in_=v_table[0][:].indirect(list1[:]))
         quantize(moving[0][0][:], moving[0][1][:], stage[0][:])
         nc.vector.tensor_copy(out=v_codes[1][:], in_=v_table[1][:].indirect(list1[:]))
         quantize(moving[1][0][:], moving[1][1][:], stage[1][:])
         for u in by_slot[4:]:
-            scatter(u, list4, wg2_sb)
+            put_h2(u)
 
-        load_rows(raw0, w1, PASS, HALF)
+        load_rows(raw0, w1, PASS, BANK)
         load_rows(raw1, plan, 0, 0)
+
+        turns4 = turns[:].rearrange("j (t g p) -> j t g p", t=PACK, g=GROUPS)
 
         def to_turns(g, slots):
             nc.scalar.activation(
@@ -247,23 +263,25 @@ def tile_list_cavern_creep_page_kernel(
                 func=ACT.Copy, scale=1.0 / (2.0 * math.pi),
             )
 
-        def sine(u):
+        def sine(u, minus_whole):
             t = u % PACK
-            part = cols(t * S, S)
+            slot_turns = turns[:, cols(t * S, S)]
             count = rounded[t % 2]
-            nc.scalar.activation(out=count[:], in_=turns[:, part], func=ACT.Copy, bias=ROUNDER)
-            nc.scalar.activation(out=whole[:, part], in_=count[:], func=ACT.Copy, scale=-1.0, bias=ROUNDER)
-            for g in range(4):
-                for src, first in ((turns4, True), (whole4, False)):
+            nc.scalar.activation(out=count[:], in_=slot_turns, func=ACT.Copy, bias=ROUNDER)
+            nc.scalar.activation(out=minus_whole, in_=count[:], func=ACT.Copy, scale=-1.0, bias=ROUNDER)
+            for g in range(GROUPS):
+                for src, first in ((slot_turns, True), (minus_whole, False)):
                     nc.tensor.matmul(
-                        out=banks_b[t][:, cols(P * g, P)], lhsT=src[:, t, g, :], rhs=ident[:],
+                        out=banks_b[t][:, cols(P * g, P)], lhsT=src[:, cols(P * g, P)], rhs=ident[:],
                         start=first, stop=not first, is_transpose=True,
                     )
-            nc.scalar.activation(out=whole[:, part], in_=banks_b[t][:], func=ACT.Sin, scale=2.0 * math.pi)
-            nc.scalar.activation(out=h_slot(u), in_=whole[:, part], func=ACT.Copy, scale=gain_sb[:, u : u + 1])
+            nc.scalar.activation(out=h_slot(u), in_=banks_b[t][:], func=ACT.Sin, scale=2.0 * math.pi)
 
-        def sines(b):
-            for g in range(4):
+        def spare_slot(u):
+            return spare[:, cols(u % PACK * S, S)]
+
+        def arguments(b):
+            for g in range(GROUPS):
                 for a in range(2):
                     codes, scales = moving[2 * b + a]
                     nc.tensor.matmul_mx(
@@ -276,50 +294,66 @@ def tile_list_cavern_creep_page_kernel(
                         stop=(a == 1),
                     )
                 to_turns(g, slice(0, 1))
-            sine(PACK * b)
-            for g in range(4):
+
+        def other_slots():
+            for g in range(GROUPS):
                 to_turns(g, slice(1, PACK))
-            sine(PACK * b + 1)
 
         def widen(u):
-            nc.scalar.copy(out=base_wide[:, cols(u * HALF, HALF)], in_=base_sb[:, u : u + 1].to_broadcast([P, HALF]))
+            nc.scalar.copy(out=base_wide[:, cols(u * BANK, BANK)], in_=base_sb[:, u : u + 1].to_broadcast([P, BANK]))
 
-        sines(0)
+        arguments(0)
+        sine(0, spare_slot(0))
+        turn(wg1_natural)
+        for t in range(PACK):
+            repeat(t, 1)
+        for t in range(PACK):
+            bank = turn_back(t)
+            for u in (t, PACK + t):
+                nc.scalar.activation(
+                    out=wg1_gain[:, cols(u * S, S)], in_=bank[:], func=ACT.Copy, scale=gain_sb[:, u : u + 1]
+                )
+        other_slots()
+        sine(1, spare_slot(1))
         for u in range(2):
             widen(u)
         for i, raw in enumerate((raw2, raw0)):
             weave(stage[i][:], raw[:], 2)
             quantize(moving[2 + i][0][:], moving[2 + i][1][:], stage[i][:])
-        for u in range(2, 4):
-            sine(u)
-        for u in range(2, 8):
-            widen(u)
+        sine(2, raw0[:, cols(0, S)])
+        widen(2)
+        sine(3, spare_slot(3))
+        widen(3)
 
-        load_rows(raw2, plan, 0, HALF)
+        load_rows(raw2, plan, 0, BANK)
         load_words(w4_codes, w4_words[0])
         load_plane(w4_plane, w4_scales)
         load_rows(raw0, w3, 0, 0)
 
-        x_first = [held("x_first%d" % i, PACK * HALF, F32, "shared%d" % (i + 1)) for i in range(2)]
-        for u in range(4):
-            scatter(u, list3, wg1_sb)
+        x_first = [held("x_first%d" % i, PACK * BANK, F32, "shared%d" % (i + 1)) for i in range(2)]
+        for u in range(PACK):
+            put_h1(u)
             for half in range(2):
-                fetch(u, x_first[half][:, cols(u * HALF, HALF)], half * HALF, HALF)
+                fetch(u, x_first[half][:, cols(u * BANK, BANK)], half * BANK, BANK)
 
         for half, raw in enumerate((raw1, raw2)):
-            weave(stage[half][:], raw[:], 2)
+            weave(stage[half][:], raw[:], 1)
             quantize(plan_q[half][0][:], plan_q[half][1][:], stage[half][:])
         load_rows(raw1, w3, PASS, 0)
-        sines(1)
-        for u in range(6, 8):
-            sine(u)
-        for u in range(4, 8):
-            scatter(u, list3, wg1_sb)
+        arguments(1)
+        sine(PACK, raw2[:, cols(0, S)])
+        other_slots()
+        for u in range(PACK + 1, TILES):
+            sine(u, spare_slot(u))
+        for u in range(PACK, TILES):
+            widen(u)
+        for u in range(PACK, TILES):
+            put_h1(u)
         for b, raw in enumerate((raw0, raw1)):
-            weave(stage[b][:], raw[:], 2)
+            weave(stage[b][:], raw[:], 1)
             quantize(w3_q[b][0][:], w3_q[b][1][:], stage[b][:])
 
-        woven_first = [whole[:, cols(half * 2 * S, 2 * S)].bitcast(BF16) for half in range(2)]
+        woven_first = [spare[:, cols(half * 2 * S, 2 * S)].bitcast(BF16) for half in range(2)]
         for half in range(2):
             weave(woven_first[half], x_first[half][:], 1)
 
@@ -335,7 +369,7 @@ def tile_list_cavern_creep_page_kernel(
                     start=True,
                     stop=True,
                 )
-                nc.scalar.activation(out=gates[half][:, cols(n * HALF, HALF)], in_=banks_b[n][:], func=ACT.Sigmoid)
+                nc.scalar.activation(out=gates[half][:, cols(n * BANK, BANK)], in_=banks_b[n][:], func=ACT.Sigmoid)
 
         def score_pass(dst, n, b, codes, scales):
             nc.tensor.matmul_mx(
@@ -348,52 +382,52 @@ def tile_list_cavern_creep_page_kernel(
                 stop=(b == 1),
             )
 
-        x_third = x_first[0][:, cols(0, PACK * QUARTER)]
-        x_fourth = x_first[1][:, cols(0, PACK * QUARTER)]
-        woven_third = x_first[1][:, cols(QUARTER // 2, 2 * QUARTER)].bitcast(BF16)
-        woven_fourth = stage[1][:, cols(0, PACK * QUARTER)]
+        x_third = x_first[0][:, cols(0, PACK * HALF_BANK)]
+        x_fourth = x_first[1][:, cols(0, PACK * HALF_BANK)]
+        woven_third = x_first[1][:, cols(HALF_BANK // 2, 2 * HALF_BANK)].bitcast(BF16)
+        woven_fourth = stage[1][:, cols(0, PACK * HALF_BANK)]
 
         quantize(moving[0][0][:], moving[0][1][:], woven_first[0])
         for t in range(PACK):
-            fetch(4 + t, x_third[:, cols(t * QUARTER, QUARTER)], HALF, QUARTER)
+            fetch(PACK + t, x_third[:, cols(t * HALF_BANK, HALF_BANK)], BANK, HALF_BANK)
         quantize(moving[1][0][:], moving[1][1][:], woven_first[1])
         for t in range(PACK):
-            fetch(4 + t, whole[:, cols(t * HALF, HALF)], 0, HALF)
+            fetch(PACK + t, spare_slot(t), 0, BANK)
         for n in range(4):
             score_pass(banks_b[n][:], n, 0, moving[0][0][:], moving[0][1][:])
 
-        def quarter(i, woven):
-            part = cols(i * QUARTER, QUARTER)
+        def score_quarter(i, woven):
+            part = cols(i * HALF_BANK, HALF_BANK)
             quantize(moving[3][0][:, part], moving[3][1][:, part], woven)
             for n in range(4):
-                dst = banks_a[2 * i + n // 2][:, cols((n % 2) * QUARTER, QUARTER)]
+                dst = banks_a[2 * i + n // 2][:, cols((n % 2) * HALF_BANK, HALF_BANK)]
                 score_pass(dst, n, 0, moving[1][0][:, part], moving[1][1][:, part])
                 score_pass(dst, n, 1, moving[3][0][:, part], moving[3][1][:, part])
 
-        def finish_quarter(i):
+        def store_quarter(i):
             gate = gates[1][:].rearrange("p (n c) -> p n c", n=4)
             for pair in range(2):
-                slot = 2 * i + pair
-                result = h_slot(4 + slot).rearrange("p (n c) -> p n c", n=2)
+                which = 2 * i + pair
+                result = h_slot(PACK + which).rearrange("p (n c) -> p n c", n=2)
                 nc.vector.tensor_tensor(
-                    result, banks_a[slot][:].rearrange("p (n c) -> p n c", n=2),
-                    gate[:, cols(2 * pair, 2), cols(i * QUARTER, QUARTER)], ALU.mult,
+                    result, banks_a[which][:].rearrange("p (n c) -> p n c", n=2),
+                    gate[:, cols(2 * pair, 2), cols(i * HALF_BANK, HALF_BANK)], ALU.mult,
                 )
-                dst = out[cols(2 * P * pair, 2 * P), cols(HALF + i * QUARTER, QUARTER)]
+                dst = out[cols(2 * P * pair, 2 * P), cols(BANK + i * HALF_BANK, HALF_BANK)]
                 nc.sync.dma_start(out=dst.rearrange("(n p) c -> p n c", p=P), in_=result)
 
         weave(woven_third, x_third, 1)
-        quarter(0, woven_third)
-        weave(stage[0][:], whole[:], 1)
+        score_quarter(0, woven_third)
+        weave(stage[0][:], spare[:], 1)
         for t in range(PACK):
-            fetch(4 + t, x_fourth[:, cols(t * QUARTER, QUARTER)], HALF + QUARTER, QUARTER)
+            fetch(PACK + t, x_fourth[:, cols(t * HALF_BANK, HALF_BANK)], BANK + HALF_BANK, HALF_BANK)
         quantize(moving[2][0][:], moving[2][1][:], stage[0][:])
         for n in range(4):
             score_pass(banks_b[n][:], n, 1, moving[2][0][:], moving[2][1][:])
-        finish_quarter(0)
+        store_quarter(0)
         weave(woven_fourth, x_fourth, 1)
-        quarter(1, woven_fourth)
+        score_quarter(1, woven_fourth)
         for n in range(4):
-            nc.vector.tensor_tensor(h_slot(n), banks_b[n][:], gates[0][:, cols(n * HALF, HALF)], ALU.mult)
-            nc.sync.dma_start(out=out[cols(P * n, P), cols(0, HALF)], in_=h_slot(n))
-        finish_quarter(1)
+            nc.vector.tensor_tensor(h_slot(n), banks_b[n][:], gates[0][:, cols(n * BANK, BANK)], ALU.mult)
+            nc.sync.dma_start(out=out[cols(P * n, P), cols(0, BANK)], in_=h_slot(n))
+        store_quarter(1)

import math
from contextlib import ExitStack

import concourse.mybir as mybir
from concourse.masks import make_identity

K, M, H, N, T, S, T2, J = 1024, 512, 1024, 512, 2048, 512, 2048, 1024
FLOPS = 2 * (K * H * S + M * H * S + H * N * J + M * N * J)

F32 = mybir.dt.float32
BF16 = mybir.dt.bfloat16
I32 = mybir.dt.int32
U32 = mybir.dt.uint32
U16 = mybir.dt.uint16
U8 = mybir.dt.uint8
FP8X4 = mybir.dt.float8_e4m3fn_x4
FP4X4 = mybir.dt.float4_e2m1fn_x4
ACT = mybir.ActivationFunctionType
ALU = mybir.AluOpType

P = 128
PACK = 4
PASS = P * PACK
TILES = H // P
BANK = 512
HALF_BANK = 256
GROUPS = BANK // P
QUADRANT = 32
ROUNDER = 1.5 * 2.0**23


def tile_list_cavern_creep_page_kernel(
    tc, tab_words, tab_scales, offs, tab2_words, tab2_scales, offs2, w1, gain, w2_words, w2_scales,
    page0, wg1, wg2, offs3, offs4, offs5, base, w3, plan, w4_words, w4_scales, out,
):
    nc = tc.nc
    with ExitStack() as ctx:
        sb = ctx.enter_context(tc.tile_pool(name="sb", bufs=1))
        ps = ctx.enter_context(tc.psum_pool(name="ps", bufs=1))

        def held(name, width, dtype, tag=""):
            return sb.tile([P, width], dtype, name=name, tag=tag or name, align_bytes=64)

        def cols(start, width):
            return slice(start, start + width)

        list1 = sb.tile([P, S // 16], U16, name="list1")
        list2 = sb.tile([P, S // 16], U16, name="list2")
        list3 = sb.tile([P, S // 16], U16, name="list3")
        list4 = sb.tile([P, S // 16], U16, name="list4")
        list5 = sb.tile([P, J // 16], U16, name="list5")

        banks_a = [ps.tile([P, BANK], F32, name="bank_a%d" % i) for i in range(4)]
        banks_b = [ps.tile([P, BANK], F32, name="bank_b%d" % i) for i in range(4)]

        pages = [held("page%d" % u, T2, F32) for u in range(TILES)]
        v2_table = held("v2_table", T, U32, "shared0")
        v_table = [held("v_table%d" % a, T, U32, "shared%d" % (a + 1)) for a in range(2)]
        v2_table_scales = held("v2_table_scales", T, U8)
        v_table_scales = held("v_table_scales", T, U8)
        v2_codes = held("v2_codes", S, U32)
        v2_scales = held("v2_scales", S, U8)
        v_codes = [held("v_codes%d" % a, S, U32) for a in range(2)]
        v_scales = held("v_scales", S, U8)
        w2_raw = held("w2_raw", 2 * H, U8)
        w2_raw_scales = held("w2_raw_scales", H, U8)
        w2_codes = held("w2_codes", 2 * H, U8)
        w2_dealt_scales = held("w2_dealt_scales", H, U8)
        w4_codes = held("w4_codes", N, U32)
        w4_plane = held("w4_plane", N, U8)
        wg1_gain = held("wg1_gain", TILES * S, F32)
        wg2_dealt = held("wg2_dealt", PACK * S, F32)
        gain_sb = held("gain_sb", TILES, F32)
        base_sb = held("base_sb", TILES, F32)
        base_wide = held("base_wide", TILES * BANK, F32)
        ident = held("ident", P, F32)
        warm = held("warm", 1, F32)
        raw0 = held("raw0", PACK * BANK, F32)
        raw1 = held("raw1", PACK * BANK, F32)
        stage = [held("stage%d" % i, PACK * BANK, BF16) for i in range(2)]
        moving = [(held("moving_codes%d" % i, BANK, U32), held("moving_scales%d" % i, BANK, U8)) for i in range(4)]
        w3_q = [(held("w3_codes%d" % i, N, U32), held("w3_scales%d" % i, N, U8)) for i in range(2)]
        plan_q = [(held("plan_codes%d" % i, BANK, U32), held("plan_scales%d" % i, BANK, U8)) for i in range(2)]
        h_sb = held("h_sb", TILES * S, F32)
        turns = held("turns", PACK * S, F32)
        repeated = held("repeated", PACK * S, F32)
        spare = held("spare", PACK * S, F32)
        rounded = [held("rounded%d" % i, S, U32) for i in range(2)]

        def load(dst, src):
            nc.sync.dma_start(out=dst, in_=src)

        def load_words(dst, words):
            load(dst[:].bitcast(I32), words.rearrange("p t i -> p (t i)").bitcast(I32))

        def load_plane(dst, scales):
            passes = scales.shape[0]
            for q in range(4):
                rows = cols(QUADRANT * q, 4 * passes)
                load(dst[rows, :].bitcast(I32), scales[:, cols(4 * q, 4), :].bitcast(I32))

        def load_page(u):
            b, t = divmod(u, PACK)
            load(pages[u][:], page0[cols(PASS * b, PASS), :].rearrange("(p t) c -> p t c", t=PACK)[:, t, :])

        def load_vector(dst, vec):
            load(dst[:].rearrange("p (b t) -> p b t", t=PACK), vec.rearrange("(b p t) -> p b t", p=P, t=PACK))

        def load_rows(dst, matrix, row0, col0):
            src = matrix[cols(row0, PASS), cols(col0, BANK)].rearrange("(p t) c -> p t c", t=PACK)
            load(dst[:].rearrange("p (t c) -> p t c", t=PACK), src)

        def weave(dst, src, parts):
            src4 = src.rearrange("p (t c i) -> p c t i", t=PACK, i=4)
            dst4 = dst.rearrange("p (c i t) -> p c t i", t=PACK, i=4)
            step = src4.shape[1] // parts
            for part in range(parts):
                nc.scalar.copy(out=dst4[:, cols(part * step, step)], in_=src4[:, cols(part * step, step)])

        def quantize(codes, scales, woven):
            nc.vector.quantize_mx(out=codes.bitcast(FP8X4), scales=scales, in_=woven)

        def entries(offsets, j0, width):
            return offsets[:, cols(j0 // 16, width // 16)]

        def h_slot(u):
            return h_sb[:, cols(u * S, S)]

        def put(u, offsets, factors, j0, width):
            part = cols(j0, width)
            window = pages[u][:].indirect(entries(offsets, j0, width))
            nc.vector.tensor_tensor(window, h_slot(u)[:, part], factors[:, part], ALU.mult)

        def put_h2(u, j0=0, width=S):
            put(u, list4, wg2_dealt[:, cols(u % PACK * S, S)], j0, width)

        def put_h1(u):
            put(u, list3, wg1_gain[:, cols(u * S, S)], 0, S)

        def fetch(u, dst, j0, width):
            window = pages[u][:].indirect(entries(list5, j0, width))
            nc.vector.tensor_tensor(dst, window, base_wide[:, cols(u * BANK, width)], ALU.subtract)

        def turn(natural):
            for g in range(GROUPS):
                nc.tensor.transpose(banks_b[3][:, cols(P * g, P)], natural[:, cols(P * g, P)], ident[:])

        def repeat(t0, count):
            src = banks_b[3][:].rearrange("j (g m t) -> j t g m", g=GROUPS, t=PACK)[:, cols(t0, count)]
            dst = repeated[:].rearrange("j (t g q m) -> j t g q m", t=PACK, g=GROUPS, q=4)[:, cols(t0, count)]
            nc.scalar.copy(out=dst, in_=src.unsqueeze(3).to_broadcast([P, count, GROUPS, 4, QUADRANT]))

        def turn_back(t):
            bank = banks_b[1 + t % 2]
            for g in range(GROUPS):
                nc.tensor.transpose(bank[:, cols(P * g, P)], repeated[:, cols(t * S + P * g, P)], ident[:])
            return bank

        nc.gpsimd.memset(v2_table_scales[:].bitcast(I32), 0)
        nc.gpsimd.memset(w2_raw_scales[:].bitcast(I32), 0)
        nc.vector.memset(v_table_scales[:].bitcast(I32), 0)
        nc.vector.memset(w4_plane[:].bitcast(I32), 0)
        make_identity(nc, ident[:])
        nc.scalar.activation(out=warm[:], in_=ident[:, 0:1], func=ACT.Sqrt)

        load(list2[:], offs2)
        load(w2_raw[:].bitcast(I32), w2_words[0].bitcast(I32))
        load_plane(v2_table_scales, tab2_scales)
        load(spare[:, cols(0, S)], wg2)
        load_words(v2_table, tab2_words[0])
        load_plane(w2_raw_scales, w2_scales)
        load_page(0)
        load(list4[:], offs4)

        nc.vector.tensor_copy(out=v2_scales[:], in_=v2_table_scales[:].indirect(list2[:]))
        nc.vector.tensor_copy(
            out=w2_codes[:].bitcast(U16).rearrange("p (b t m) -> p b t m", b=2, t=PACK),
            in_=w2_raw[:].bitcast(U16).rearrange("p (b m t) -> p b t m", b=2, t=PACK),
        )
        for half, slots in enumerate((slice(0, 1), slice(1, PACK))):
            j0 = half * HALF_BANK
            nc.vector.tensor_copy(
                out=v2_codes[:, cols(j0, HALF_BANK)], in_=v2_table[:].indirect(entries(list2, j0, HALF_BANK))
            )
            nc.vector.tensor_copy(
                out=w2_dealt_scales[:].rearrange("p (b t m) -> p b t m", b=2, t=PACK)[:, :, slots, :],
                in_=w2_raw_scales[:].rearrange("p (b m t) -> p b t m", b=2, t=PACK)[:, :, slots, :],
            )

        by_slot = [PACK * b + t for t in range(PACK) for b in range(2)]

        def root(i, j0, width):
            u = by_slot[i]
            part = cols(j0, width)
            bank = banks_a[(i + j0 // width) % 4][:, part]
            nc.tensor.matmul_mx(
                out=bank,
                lhsT=w2_codes[:, cols(2 * P * u, 2 * P)].bitcast(FP4X4),
                lhsT_scale=w2_dealt_scales[:, cols(P * u, P)],
                rhs=v2_codes[:, part].bitcast(FP8X4),
                rhs_scale=v2_scales[:, part],
                start=True,
                stop=True,
            )
            nc.scalar.activation(out=h_slot(u)[:, part], in_=bank, func=ACT.Abs)
            nc.scalar.activation(out=h_slot(u)[:, part], in_=h_slot(u)[:, part], func=ACT.Sqrt)

        turn(spare[:, cols(0, S)])
        repeat(0, 1)
        nc.scalar.copy(out=wg2_dealt[:, cols(0, S)], in_=turn_back(0)[:])
        for j0 in (0, HALF_BANK):
            root(0, j0, HALF_BANK)
        root(1, 0, S)
        repeat(1, PACK - 1)
        for t in range(1, PACK):
            nc.scalar.copy(out=wg2_dealt[:, cols(t * S, S)], in_=turn_back(t)[:])
        for i in range(2, TILES):
            root(i, 0, S)

        raw2 = held("raw2", PACK * BANK, F32, "shared0")

        for u in by_slot[1:4]:
            load_page(u)
        load_rows(raw0, w1, 0, 0)
        load(list1[:], offs)
        load_plane(v_table_scales, tab_scales)
        load_words(v_table[0], tab_words[0])
        load_rows(raw1, w1, PASS, 0)
        load_words(v_table[1], tab_words[1])
        wg1_natural = spare[:, cols(3 * S, S)]
        load(wg1_natural, wg1)
        load_vector(gain_sb, gain)
        for u in by_slot[4:]:
            load_page(u)
        load(list3[:], offs3)
        load(list5[:], offs5)
        load_vector(base_sb, base)
        load_rows(raw2, w1, 0, BANK)

        for j0 in (0, HALF_BANK):
            put_h2(0, j0, HALF_BANK)
        for u in by_slot[1:4]:
            put_h2(u)
        weave(stage[0][:], raw0[:], 2)
        weave(stage[1][:], raw1[:], 2)
        nc.scalar.activation(out=warm[:], in_=h_slot(by_slot[-1])[:, 0:1], func=ACT.Sin, scale=0.0)
        nc.vector.tensor_copy(out=v_scales[:], in_=v_table_scales[:].indirect(list1[:]))
        nc.vector.tensor_copy(out=v_codes[0][:], in_=v_table[0][:].indirect(list1[:]))
        quantize(moving[0][0][:], moving[0][1][:], stage[0][:])
        nc.vector.tensor_copy(out=v_codes[1][:], in_=v_table[1][:].indirect(list1[:]))
        quantize(moving[1][0][:], moving[1][1][:], stage[1][:])
        for u in by_slot[4:]:
            put_h2(u)

        load_rows(raw0, w1, PASS, BANK)
        load_rows(raw1, plan, 0, 0)

        turns4 = turns[:].rearrange("j (t g p) -> j t g p", t=PACK, g=GROUPS)

        def to_turns(g, slots):
            nc.scalar.activation(
                out=turns4[:, slots, g, :], in_=banks_a[g][:].rearrange("j (p t) -> j t p", t=PACK)[:, slots, :],
                func=ACT.Copy, scale=1.0 / (2.0 * math.pi),
            )

        def sine(u, minus_whole):
            t = u % PACK
            slot_turns = turns[:, cols(t * S, S)]
            count = rounded[t % 2]
            nc.scalar.activation(out=count[:], in_=slot_turns, func=ACT.Copy, bias=ROUNDER)
            nc.scalar.activation(out=minus_whole, in_=count[:], func=ACT.Copy, scale=-1.0, bias=ROUNDER)
            for g in range(GROUPS):
                for src, first in ((slot_turns, True), (minus_whole, False)):
                    nc.tensor.matmul(
                        out=banks_b[t][:, cols(P * g, P)], lhsT=src[:, cols(P * g, P)], rhs=ident[:],
                        start=first, stop=not first, is_transpose=True,
                    )
            nc.scalar.activation(out=h_slot(u), in_=banks_b[t][:], func=ACT.Sin, scale=2.0 * math.pi)

        def spare_slot(u):
            return spare[:, cols(u % PACK * S, S)]

        def arguments(b):
            for g in range(GROUPS):
                for a in range(2):
                    codes, scales = moving[2 * b + a]
                    nc.tensor.matmul_mx(
                        out=banks_a[g][:],
                        lhsT=v_codes[a][:, cols(P * g, P)].bitcast(FP8X4),
                        lhsT_scale=v_scales[4 * a : P, cols(P * g, P)],
                        rhs=codes[:].bitcast(FP8X4),
                        rhs_scale=scales[:],
                        start=(a == 0),
                        stop=(a == 1),
                    )
                to_turns(g, slice(0, 1))

        def other_slots():
            for g in range(GROUPS):
                to_turns(g, slice(1, PACK))

        def widen(u):
            nc.scalar.copy(out=base_wide[:, cols(u * BANK, BANK)], in_=base_sb[:, u : u + 1].to_broadcast([P, BANK]))

        arguments(0)
        sine(0, spare_slot(0))
        turn(wg1_natural)
        for t in range(PACK):
            repeat(t, 1)
        for t in range(PACK):
            bank = turn_back(t)
            for u in (t, PACK + t):
                nc.scalar.activation(
                    out=wg1_gain[:, cols(u * S, S)], in_=bank[:], func=ACT.Copy, scale=gain_sb[:, u : u + 1]
                )
        other_slots()
        sine(1, spare_slot(1))
        for u in range(2):
            widen(u)
        for i, raw in enumerate((raw2, raw0)):
            weave(stage[i][:], raw[:], 2)
            quantize(moving[2 + i][0][:], moving[2 + i][1][:], stage[i][:])
        sine(2, raw0[:, cols(0, S)])
        widen(2)
        sine(3, spare_slot(3))
        widen(3)

        load_rows(raw2, plan, 0, BANK)
        load_words(w4_codes, w4_words[0])
        load_plane(w4_plane, w4_scales)
        load_rows(raw0, w3, 0, 0)

        x_first = [held("x_first%d" % i, PACK * BANK, F32, "shared%d" % (i + 1)) for i in range(2)]
        for u in range(PACK):
            put_h1(u)
            for half in range(2):
                fetch(u, x_first[half][:, cols(u * BANK, BANK)], half * BANK, BANK)

        for half, raw in enumerate((raw1, raw2)):
            weave(stage[half][:], raw[:], 1)
            quantize(plan_q[half][0][:], plan_q[half][1][:], stage[half][:])
        load_rows(raw1, w3, PASS, 0)
        arguments(1)
        sine(PACK, raw2[:, cols(0, S)])
        other_slots()
        for u in range(PACK + 1, TILES):
            sine(u, spare_slot(u))
        for u in range(PACK, TILES):
            widen(u)
        for u in range(PACK, TILES):
            put_h1(u)
        for b, raw in enumerate((raw0, raw1)):
            weave(stage[b][:], raw[:], 1)
            quantize(w3_q[b][0][:], w3_q[b][1][:], stage[b][:])

        woven_first = [spare[:, cols(half * 2 * S, 2 * S)].bitcast(BF16) for half in range(2)]
        for half in range(2):
            weave(woven_first[half], x_first[half][:], 1)

        gates = [turns, raw2]
        for half in range(2):
            for n in range(4):
                nc.tensor.matmul_mx(
                    out=banks_b[n][:],
                    lhsT=w4_codes[:, cols(P * n, P)].bitcast(FP8X4),
                    lhsT_scale=w4_plane[:, cols(P * n, P)],
                    rhs=plan_q[half][0][:].bitcast(FP8X4),
                    rhs_scale=plan_q[half][1][:],
                    start=True,
                    stop=True,
                )
                nc.scalar.activation(out=gates[half][:, cols(n * BANK, BANK)], in_=banks_b[n][:], func=ACT.Sigmoid)

        def score_pass(dst, n, b, codes, scales):
            nc.tensor.matmul_mx(
                out=dst,
                lhsT=w3_q[b][0][:, cols(P * n, P)].bitcast(FP8X4),
                lhsT_scale=w3_q[b][1][:, cols(P * n, P)],
                rhs=codes.bitcast(FP8X4),
                rhs_scale=scales,
                start=(b == 0),
                stop=(b == 1),
            )

        x_third = x_first[0][:, cols(0, PACK * HALF_BANK)]
        x_fourth = x_first[1][:, cols(0, PACK * HALF_BANK)]
        woven_third = x_first[1][:, cols(HALF_BANK // 2, 2 * HALF_BANK)].bitcast(BF16)
        woven_fourth = stage[1][:, cols(0, PACK * HALF_BANK)]

        quantize(moving[0][0][:], moving[0][1][:], woven_first[0])
        for t in range(PACK):
            fetch(PACK + t, x_third[:, cols(t * HALF_BANK, HALF_BANK)], BANK, HALF_BANK)
        quantize(moving[1][0][:], moving[1][1][:], woven_first[1])
        for t in range(PACK):
            fetch(PACK + t, spare_slot(t), 0, BANK)
        for n in range(4):
            score_pass(banks_b[n][:], n, 0, moving[0][0][:], moving[0][1][:])

        def score_quarter(i, woven):
            part = cols(i * HALF_BANK, HALF_BANK)
            quantize(moving[3][0][:, part], moving[3][1][:, part], woven)
            for n in range(4):
                dst = banks_a[2 * i + n // 2][:, cols((n % 2) * HALF_BANK, HALF_BANK)]
                score_pass(dst, n, 0, moving[1][0][:, part], moving[1][1][:, part])
                score_pass(dst, n, 1, moving[3][0][:, part], moving[3][1][:, part])

        def store_quarter(i):
            gate = gates[1][:].rearrange("p (n c) -> p n c", n=4)
            for pair in range(2):
                which = 2 * i + pair
                result = h_slot(PACK + which).rearrange("p (n c) -> p n c", n=2)
                nc.vector.tensor_tensor(
                    result, banks_a[which][:].rearrange("p (n c) -> p n c", n=2),
                    gate[:, cols(2 * pair, 2), cols(i * HALF_BANK, HALF_BANK)], ALU.mult,
                )
                dst = out[cols(2 * P * pair, 2 * P), cols(BANK + i * HALF_BANK, HALF_BANK)]
                nc.sync.dma_start(out=dst.rearrange("(n p) c -> p n c", p=P), in_=result)

        weave(woven_third, x_third, 1)
        score_quarter(0, woven_third)
        weave(stage[0][:], spare[:], 1)
        for t in range(PACK):
            fetch(PACK + t, x_fourth[:, cols(t * HALF_BANK, HALF_BANK)], BANK + HALF_BANK, HALF_BANK)
        quantize(moving[2][0][:], moving[2][1][:], stage[0][:])
        for n in range(4):
            score_pass(banks_b[n][:], n, 1, moving[2][0][:], moving[2][1][:])
        store_quarter(0)
        weave(woven_fourth, x_fourth, 1)
        score_quarter(1, woven_fourth)
        for n in range(4):
            nc.vector.tensor_tensor(h_slot(n), banks_b[n][:], gates[0][:, cols(n * BANK, BANK)], ALU.mult)
            nc.sync.dma_start(out=out[cols(P * n, P), cols(0, BANK)], in_=h_slot(n))
        store_quarter(1)
